import numpy as np
import ml_dtypes


def mxq(x, axis, fmt="e4m3"):
    dtype, down = {"e4m3": (ml_dtypes.float8_e4m3fn, 7), "e5m2": (ml_dtypes.float8_e5m2, 14)}[fmt]
    v = np.moveaxis(np.asarray(x, np.float32).astype(ml_dtypes.bfloat16).astype(np.float64), axis, -1)
    blocks = v.reshape(v.shape[:-1] + (-1, 32))
    amax = np.abs(blocks).max(-1, keepdims=True)
    byte = np.maximum(np.where(amax > 0, np.frexp(amax)[1] - 1 + 127, 0) - down, 1)
    scale = np.exp2(byte - 127.0)
    codes = (blocks / scale).astype(np.float32).astype(dtype).astype(np.float64)
    return np.moveaxis((codes * scale).reshape(v.shape), -1, axis)


WIDE = False


def mx_kscale(k):
    if not WIDE:
        return np.ones(k)
    levels = np.array([10, -10, 5, -5, 0])
    if k % 512:
        return np.exp2(np.random.permutation(np.resize(levels, k // 32))).repeat(32)
    a = np.empty((k // 512, 16))
    for p in range(k // 512):
        a[p, :8] = np.random.permutation(np.resize(levels, 8))
        for g in range(8):
            far = levels[np.abs(levels - a[p, g]) >= 10]
            a[p, g + 8] = far[np.random.randint(len(far))]
    return np.exp2(a.ravel()).repeat(32)


def f64(x):
    return np.asarray(x).astype(np.float64)


def striped(idx):
    return np.tile(idx.reshape(-1, 16).T, (8, 1)).astype(np.uint16)


def unstriped(offs):
    return offs[:16].T.reshape(-1).astype(np.int64)


def striped8(idx):
    return np.concatenate([x.reshape(-1, 16).T for x in idx]).astype(np.uint16)


def runs(offs, k):
    lists = np.stack([offs[16 * r : 16 * r + 16].T.reshape(-1) for r in range(8)]).astype(np.int64)
    return lists[np.arange(k) % 512 // 64]


def pack_weight(w):
    k, n = w.shape
    w = f64(np.asarray(w, np.float32).astype(ml_dtypes.bfloat16)).reshape(k // 32, 32, n)
    amax = np.abs(w).max(1)
    byte = np.clip(np.where(amax > 0, np.frexp(amax)[1] - 1 + 127 - 7, 1), 1, 254)
    scaled = (w * np.exp2(127.0 - byte)[:, None, :]).reshape(k, n).astype(np.float32)
    words = np.ascontiguousarray(scaled.reshape(k // 512, 128, 4, n).transpose(0, 1, 3, 2)).astype(ml_dtypes.float8_e4m3fn).view(np.uint8)
    return words, np.ascontiguousarray(byte.astype(np.uint8).reshape(k // 512, 16, n))


def unpack_weight(words, scales):
    g, p, n, _ = words.shape
    vals = np.ascontiguousarray(words).view(ml_dtypes.float8_e4m3fn).astype(np.float64) * np.repeat(np.exp2(scales.astype(np.float64) - 127.0), 8, axis=1)[..., None]
    return vals.transpose(0, 1, 3, 2).reshape(g * 512, n)


def relu(v):
    return np.maximum(v, 0.0)


K, T, S, V, H = 512, 2048, 512, 512, 512


def setup_inputs():
    n = np.random.standard_normal
    s = mx_kscale(K)[:, None]
    u = mx_kscale(S)
    packed_xT = pack_weight(n((K, T)) * s)
    return {
        "x_words": packed_xT[0],
        "x_scales": packed_xT[1],
        "w1": (n((K, H)) / np.sqrt(K) / s).astype(np.float32),
        "w2": (n((K, H)) / np.sqrt(K) / s).astype(np.float32),
        "ga": (np.random.uniform(0.5, 1.5, (H, 1)) * u[:, None]).astype(np.float32),
        "gb": (np.random.uniform(0.5, 1.5, (H, 1)) / u[:, None]).astype(np.float32),
        "offs": striped(np.random.permutation(T)[:S]),
        "two": striped(np.random.permutation(T)[:V]),
        "n1": striped8(np.stack([np.random.permutation(S) for _ in range(8)])),
        "n2": striped8(np.stack([np.random.permutation(S) for _ in range(8)])),
        "nq": striped8(np.stack([np.random.permutation(V) for _ in range(8)])),
    }


def reference(x_words, x_scales, w1, w2, ga, gb, offs, two, n1, n2, nq):
    xq = unpack_weight(x_words, x_scales)[:, unstriped(offs)]
    a = mxq(f64(w1), 0, "e4m3").T @ xq
    z = f64(ga) * ((a[np.arange(H)[:, None], runs(n1, H)]) * (a[np.arange(H)[:, None], runs(n2, H)]))
    x_two = unpack_weight(x_words, x_scales)[:, unstriped(two)]
    b = mxq(f64(w2), 0, "e4m3").T @ x_two
    z2 = f64(gb) * (relu(b[np.arange(H)[:, None], runs(nq, H)] - b))
    s = 0.0625 * ((mxq(z, 0, "e4m3").T @ mxq(z2, 0, "e4m3")))
    return s

@@ -1,0 +1,236 @@
+from contextlib import ExitStack
+
+import concourse.mybir as mybir
+
+K, T, S, V, H = 512, 2048, 512, 512, 512
+FLOPS = 2 * K * H * S + 2 * K * H * V + 2 * H * S * V
+
+F32 = mybir.dt.float32
+BF16 = mybir.dt.bfloat16
+I32 = mybir.dt.int32
+U32 = mybir.dt.uint32
+U16 = mybir.dt.uint16
+U8 = mybir.dt.uint8
+FP8X4 = mybir.dt.float8_e4m3fn_x4
+ALU = mybir.AluOpType
+ACT = mybir.ActivationFunctionType
+
+P = 128
+PACK = 4
+LIST_ROWS = 16
+HALF = 256
+KEY_CHUNKS = ((0, 256), (256, 256))
+QUERY_CHUNKS = ((0, 256), (256, 128), (384, 128))
+
+
+def list_slice(offsets, start, width):
+    return offsets[:, start // LIST_ROWS : (start + width) // LIST_ROWS]
+
+
+def interleaved(tile):
+    return tile[:].rearrange("p (c i) t -> p c t i", i=4)
+
+
+def by_planes(tile):
+    return tile[:].rearrange("p t (c i) -> p c t i", i=4)
+
+
+def tile_picked_keytwo_none_p_kernel(
+    tc, x_words, x_scales, w1, w2, ga, gb, offs, two, n1, n2, nq, out
+):
+    nc = tc.nc
+    with ExitStack() as ctx:
+        lists = ctx.enter_context(tc.tile_pool(name="lists", bufs=1))
+        keep = ctx.enter_context(tc.tile_pool(name="keep", bufs=1))
+        psum = ctx.enter_context(tc.psum_pool(name="psum", bufs=1))
+
+        def load_list(source, name):
+            tile = lists.tile([P, S // LIST_ROWS], U16, name=name)
+            nc.sync.dma_start(tile[:], source)
+            return tile
+
+        def load_weight_half(w, name, h):
+            rows = w.rearrange("(p j) c -> p j c", j=PACK)
+            raw = keep.tile([P, PACK, HALF], F32, name="%s_raw%d" % (name, h))
+            nc.sync.dma_start(raw[:], rows[:, :, h * HALF : (h + 1) * HALF])
+            return raw
+
+        def load_gain(g, name):
+            tile = keep.tile([P, PACK], F32, name=name)
+            nc.gpsimd.dma_start(tile[:], g.rearrange("(p t) o -> p (t o)", t=PACK))
+            return tile
+
+        def cast_weight(halves, name):
+            grouped = keep.tile([P, PACK, P, PACK], BF16, name=name + "_bf", tag=name + "_bf", align_bytes=64)
+            m_half = HALF // PACK
+            for h, raw in enumerate(halves):
+                nc.scalar.copy(
+                    grouped[:, :, h * m_half : (h + 1) * m_half, :].rearrange("p t m j -> p m j t"),
+                    raw[:].rearrange("p j (m t) -> p m j t", t=PACK),
+                )
+            return grouped
+
+        def quantize(grouped_flat, codes, scales):
+            nc.vector.quantize_mx(out=codes.bitcast(FP8X4), scales=scales, in_=grouped_flat)
+
+        def quantize_weight(grouped, name):
+            codes = keep.tile([P, H], U32, name=name + "_codes", align_bytes=64)
+            scales = keep.tile([P, H], U8, name=name + "_scales", align_bytes=64)
+            quantize(grouped[:].rearrange("p t m j -> p (t m j)"), codes[:], scales[:])
+            return codes, scales
+
+        def mx(acc, lhs, lhs_cols, rhs, rhs_cols):
+            nc.tensor.matmul_mx(
+                out=acc,
+                lhsT=lhs[0][:, lhs_cols].bitcast(FP8X4),
+                lhsT_scale=lhs[1][:, lhs_cols],
+                rhs=rhs[0][:, rhs_cols].bitcast(FP8X4),
+                rhs_scale=rhs[1][:, rhs_cols],
+                start=True,
+                stop=True,
+            )
+
+        table_scales = keep.tile([P, T], U8, name="table_scales")
+        nc.gpsimd.memset(table_scales[:].bitcast(I32), 0)
+        offs_list = load_list(offs, "offs_list")
+        two_list = load_list(two, "two_list")
+        w1_raw = [load_weight_half(w1, "w1", 0)]
+        for q in range(4):
+            nc.sync.dma_start(
+                table_scales[32 * q : 32 * q + 4, :].bitcast(I32),
+                x_scales[0, 4 * q : 4 * q + 4, :].bitcast(I32),
+            )
+        w1_raw.append(load_weight_half(w1, "w1", 1))
+        gb_raw = load_gain(gb, "gb_raw")
+        ga_raw = load_gain(ga, "ga_raw")
+        table_words = keep.tile([P, T], U32, name="table_words")
+        nc.sync.dma_start(
+            table_words[:].bitcast(I32), x_words[0].rearrange("p n t -> p (n t)").bitcast(I32)
+        )
+        n1_list = load_list(n1, "n1_list")
+        n2_list = load_list(n2, "n2_list")
+        w2_raw = [load_weight_half(w2, "w2", h) for h in range(2)]
+        nq_list = load_list(nq, "nq_list")
+
+        def pick(table, dtype, offsets, name):
+            picked = keep.tile([P, S], dtype, name=name, align_bytes=64)
+            nc.vector.tensor_copy(picked[:], table[:].indirect(offsets[:]))
+            return picked
+
+        key_scales = pick(table_scales, U8, offs_list, "key_scales")
+        query_scales = pick(table_scales, U8, two_list, "query_scales")
+
+        sign01 = keep.tile([P, PACK], F32, name="sign01")
+        sign = keep.tile([P, PACK], F32, name="sign")
+        gb_abs = keep.tile([P, PACK], F32, name="gb_abs")
+        ga_signed = keep.tile([P, PACK], F32, name="ga_signed")
+        nc.gpsimd.tensor_scalar(sign01[:], gb_raw[:], 0.0, 2.0, ALU.is_ge, ALU.mult)
+        nc.gpsimd.tensor_scalar(sign[:], sign01[:], 1.0, -1.0, ALU.mult, ALU.add)
+        nc.gpsimd.tensor_tensor(ga_signed[:], ga_raw[:], sign[:], ALU.mult)
+        nc.gpsimd.tensor_tensor(gb_abs[:], gb_raw[:], sign[:], ALU.mult)
+
+        w1_q = quantize_weight(cast_weight(w1_raw, "w1"), "w1")
+
+        ga_wide = keep.tile([P, PACK, HALF], F32, name="ga_wide")
+        nc.scalar.activation(ga_wide[:], ga_signed[:].unsqueeze(2).to_broadcast([P, PACK, HALF]), ACT.Copy)
+
+        key_words = pick(table_words, U32, offs_list, "key_words")
+        query_words = pick(table_words, U32, two_list, "query_words")
+
+        a_rows = []
+        for t in range(PACK):
+            acc = psum.tile([P, S], F32, name="acc_a%d" % t, tag="bank%d" % t)
+            mx(acc[:], w1_q, slice(t * P, (t + 1) * P), (key_words, key_scales), slice(0, S))
+            rows = keep.tile([P, S], F32, name="a_rows%d" % t)
+            nc.scalar.copy(rows[:], acc[:])
+            a_rows.append(rows)
+
+        w2_bf = cast_weight(w2_raw, "w2")
+
+        z_codes = keep.tile([P, S], U32, name="z_codes", align_bytes=64)
+        z_scales = keep.tile([P, S], U8, name="z_scales", align_bytes=64)
+
+        def key_gathers(c):
+            start, width = KEY_CHUNKS[c]
+            first = keep.tile([P, PACK, width], F32, name="first%d" % c, tag=("w1_bf", "w2_bf")[c], align_bytes=64)
+            z = keep.tile([P, PACK, width], F32, name="z%d" % c)
+            for pair in range(0, PACK, 2):
+                for t in (pair, pair + 1):
+                    nc.vector.tensor_tensor(
+                        first[:, t, :], a_rows[t][:].indirect(list_slice(n1_list, start, width)), ga_wide[:, t, :], ALU.mult
+                    )
+                for t in (pair, pair + 1):
+                    nc.vector.tensor_tensor(
+                        z[:, t, :], a_rows[t][:].indirect(list_slice(n2_list, start, width)), first[:, t, :], ALU.mult
+                    )
+            z_bf = keep.tile([P, width, PACK], BF16, name="z_bf%d" % c, tag="z_bf%d" % c, align_bytes=64)
+            nc.scalar.copy(interleaved(z_bf), by_planes(z))
+            return z_bf
+
+        def key_quantize(c, z_bf):
+            start, width = KEY_CHUNKS[c]
+            cols = slice(start, start + width)
+            quantize(z_bf[:].rearrange("p c t -> p (c t)"), z_codes[:, cols], z_scales[:, cols])
+
+        z_bf0 = key_gathers(0)
+
+        w2_q = quantize_weight(w2_bf, "w2")
+        b_rows = []
+        b_own = []
+        for t in range(PACK):
+            acc = psum.tile([P, V], F32, name="acc_b%d" % t, tag="bank%d" % (PACK + t))
+            mx(acc[:], w2_q, slice(t * P, (t + 1) * P), (query_words, query_scales), slice(0, V))
+            rows = keep.tile([P, V], F32, name="b_rows%d" % t)
+            nc.scalar.activation(rows[:], acc[:], ACT.Copy, scale=gb_abs[:, t : t + 1])
+            own = keep.tile([P, V], F32, name="b_own%d" % t)
+            nc.sync.dma_start(own[:], rows[:])
+            b_rows.append(rows)
+            b_own.append(own)
+
+        z_bf1 = key_gathers(1)
+        key_quantize(0, z_bf0)
+
+        out_rows = out.rearrange("(a p) v -> p a v", p=P)
+
+        def query_gathers(c):
+            start, width = QUERY_CHUNKS[c]
+            diff = keep.tile([P, PACK, width], F32, name="diff%d" % c, tag=("z_bf0", "z_bf1", "z2_bf0")[c], align_bytes=64)
+            for t in range(PACK):
+                nc.vector.tensor_tensor(
+                    diff[:, t, :],
+                    b_rows[t][:].indirect(list_slice(nq_list, start, width)),
+                    b_own[t][:, start : start + width],
+                    ALU.subtract,
+                )
+            z2_bf = keep.tile([P, width, PACK], BF16, name="z2_bf%d" % c, tag="z2_bf%d" % c, align_bytes=64)
+            if c == len(QUERY_CHUNKS) - 1:
+                nc.vector.tensor_scalar(interleaved(z2_bf), by_planes(diff), 0.0, None, ALU.max)
+            else:
+                nc.scalar.activation(interleaved(z2_bf), by_planes(diff), ACT.Relu)
+            return z2_bf
+
+        def query_scores(c, z2_bf):
+            start, width = QUERY_CHUNKS[c]
+            codes = keep.tile([P, width], U32, name="z2_codes%d" % c, align_bytes=64)
+            scales = keep.tile([P, width], U8, name="z2_scales%d" % c, align_bytes=64)
+            quantize(z2_bf[:].rearrange("p c t -> p (c t)"), codes[:], scales[:])
+            for half in range(2):
+                acc = psum.tile([P, 2, width], F32, name="acc_s%d_%d" % (c, half), tag="bank%d" % (2 * c + half))
+                for a in range(2):
+                    rows = slice((2 * half + a) * P, (2 * half + a + 1) * P)
+                    mx(acc[:, a, :], (z_codes, z_scales), rows, (codes, scales), slice(0, width))
+                name = "scores%d_%d" % (c, half)
+                scores = keep.tile([P, 2, width], F32, name=name, tag="z_bf1" if (c, half) == (0, 0) else name, align_bytes=64)
+                if c == len(QUERY_CHUNKS) - 1 and half == 1:
+                    nc.vector.tensor_scalar(scores[:], acc[:], 0.0625, None, ALU.mult)
+                else:
+                    nc.scalar.activation(scores[:], acc[:], ACT.Copy, scale=0.0625)
+                nc.sync.dma_start(out_rows[:, 2 * half : 2 * half + 2, start : start + width], scores[:])
+
+        z2_bf0 = query_gathers(0)
+        key_quantize(1, z_bf1)
+        z2_bf1 = query_gathers(1)
+        query_scores(0, z2_bf0)
+        z2_bf2 = query_gathers(2)
+        query_scores(1, z2_bf1)
+        query_scores(2, z2_bf2)

@@ -57,26 +57,35 @@ def tile_picked_keytwo_none_p_kernel(
 
         def load_gain(g, name):
             tile = keep.tile([P, PACK], F32, name=name)
-            nc.gpsimd.dma_start(tile[:], g.rearrange("(p t) o -> p (t o)", t=PACK))
+            nc.sync.dma_start(tile[:], g.rearrange("(p t) o -> p (t o)", t=PACK))
             return tile
 
-        def cast_weight(halves, name):
-            grouped = keep.tile([P, PACK, P, PACK], BF16, name=name + "_bf", tag=name + "_bf", align_bytes=64)
-            m_half = HALF // PACK
-            for h, raw in enumerate(halves):
-                nc.scalar.copy(
-                    grouped[:, :, h * m_half : (h + 1) * m_half, :].rearrange("p t m j -> p m j t"),
-                    raw[:].rearrange("p j (m t) -> p m j t", t=PACK),
+        def cast_weight(halves, name, tag, vector_columns):
+            grouped = keep.tile([P, PACK, P, PACK], BF16, name=name, tag=tag, align_bytes=64)
+
+            def cast(copy, first, last):
+                h, start = divmod(first, HALF)
+                copy(
+                    grouped[:, :, first // PACK : last // PACK, :].rearrange("p t m j -> p m j t"),
+                    halves[h][:, :, start : start + last - first].rearrange("p j (m t) -> p m j t", t=PACK),
                 )
+
+            cast(nc.scalar.copy, 0, HALF)
+            cast(nc.scalar.copy, HALF, H - vector_columns)
+            if vector_columns:
+                cast(nc.vector.tensor_copy, H - vector_columns, H)
             return grouped
 
         def quantize(grouped_flat, codes, scales):
             nc.vector.quantize_mx(out=codes.bitcast(FP8X4), scales=scales, in_=grouped_flat)
 
-        def quantize_weight(grouped, name):
-            codes = keep.tile([P, H], U32, name=name + "_codes", align_bytes=64)
+        def quantize_weight(grouped, name, calls):
+            codes = keep.tile([P, H], U32, name=name + "_codes", tag=name + "_codes", align_bytes=64)
             scales = keep.tile([P, H], U8, name=name + "_scales", align_bytes=64)
-            quantize(grouped[:].rearrange("p t m j -> p (t m j)"), codes[:], scales[:])
+            flat = grouped[:].rearrange("p t m j -> p (t m j)")
+            width = H // calls
+            for c in range(0, H, width):
+                quantize(flat[:, PACK * c : PACK * (c + width)], codes[:, c : c + width], scales[:, c : c + width])
             return codes, scales
 
         def mx(acc, lhs, lhs_cols, rhs, rhs_cols):
@@ -91,7 +100,7 @@ def tile_picked_keytwo_none_p_kernel(
             )
 
         table_scales = keep.tile([P, T], U8, name="table_scales")
-        nc.gpsimd.memset(table_scales[:].bitcast(I32), 0)
+        nc.vector.memset(table_scales[:].bitcast(I32), 0)
         offs_list = load_list(offs, "offs_list")
         two_list = load_list(two, "two_list")
         w1_raw = [load_weight_half(w1, "w1", 0)]
@@ -102,79 +111,88 @@ def tile_picked_keytwo_none_p_kernel(
             )
         w1_raw.append(load_weight_half(w1, "w1", 1))
         gb_raw = load_gain(gb, "gb_raw")
-        ga_raw = load_gain(ga, "ga_raw")
         table_words = keep.tile([P, T], U32, name="table_words")
         nc.sync.dma_start(
             table_words[:].bitcast(I32), x_words[0].rearrange("p n t -> p (n t)").bitcast(I32)
         )
+        ga_raw = load_gain(ga, "ga_raw")
         n1_list = load_list(n1, "n1_list")
         n2_list = load_list(n2, "n2_list")
         w2_raw = [load_weight_half(w2, "w2", h) for h in range(2)]
         nq_list = load_list(nq, "nq_list")
 
-        def pick(table, dtype, offsets, name):
+        def pick(table, dtype, offsets, name, calls):
             picked = keep.tile([P, S], dtype, name=name, align_bytes=64)
-            nc.vector.tensor_copy(picked[:], table[:].indirect(offsets[:]))
+            width = S // calls
+            for start in range(0, S, width):
+                nc.vector.tensor_copy(
+                    picked[:, start : start + width], table[:].indirect(list_slice(offsets, start, width))
+                )
             return picked
 
-        key_scales = pick(table_scales, U8, offs_list, "key_scales")
-        query_scales = pick(table_scales, U8, two_list, "query_scales")
+        key_scales = pick(table_scales, U8, offs_list, "key_scales", 1)
+        query_scales = pick(table_scales, U8, two_list, "query_scales", 1)
+        w1_q = quantize_weight(cast_weight(w1_raw, "w1_bf", "w1_bf", 0), "w1", 1)
+        key_words = pick(table_words, U32, offs_list, "key_words", 2)
+        query_words = pick(table_words, U32, two_list, "query_words", 1)
 
-        sign01 = keep.tile([P, PACK], F32, name="sign01")
+        sign3 = keep.tile([P, PACK], F32, name="sign3")
         sign = keep.tile([P, PACK], F32, name="sign")
         gb_abs = keep.tile([P, PACK], F32, name="gb_abs")
+        nc.scalar.activation(sign3[:], gb_raw[:], ACT.Sign)
+        nc.scalar.activation(gb_abs[:], gb_raw[:], ACT.Abs)
+        nc.scalar.activation(sign[:], sign3[:], ACT.Sign, bias=1.0, scale=2.0)
         ga_signed = keep.tile([P, PACK], F32, name="ga_signed")
-        nc.gpsimd.tensor_scalar(sign01[:], gb_raw[:], 0.0, 2.0, ALU.is_ge, ALU.mult)
-        nc.gpsimd.tensor_scalar(sign[:], sign01[:], 1.0, -1.0, ALU.mult, ALU.add)
-        nc.gpsimd.tensor_tensor(ga_signed[:], ga_raw[:], sign[:], ALU.mult)
-        nc.gpsimd.tensor_tensor(gb_abs[:], gb_raw[:], sign[:], ALU.mult)
+        for t in range(PACK):
+            nc.scalar.activation(ga_signed[:, t : t + 1], ga_raw[:, t : t + 1], ACT.Copy, scale=sign[:, t : t + 1])
 
-        w1_q = quantize_weight(cast_weight(w1_raw, "w1"), "w1")
-
-        ga_wide = keep.tile([P, PACK, HALF], F32, name="ga_wide")
-        nc.scalar.activation(ga_wide[:], ga_signed[:].unsqueeze(2).to_broadcast([P, PACK, HALF]), ACT.Copy)
-
-        key_words = pick(table_words, U32, offs_list, "key_words")
-        query_words = pick(table_words, U32, two_list, "query_words")
 
         a_rows = []
-        for t in range(PACK):
-            acc = psum.tile([P, S], F32, name="acc_a%d" % t, tag="bank%d" % t)
-            mx(acc[:], w1_q, slice(t * P, (t + 1) * P), (key_words, key_scales), slice(0, S))
+        a_gained = []
+
+        def project_keys(t, start, width, bank):
+            acc = psum.tile([P, width], F32, name="acc_a%d_%d" % (t, start), tag="bank%d" % bank)
+            mx(acc[:], w1_q, slice(t * P, (t + 1) * P), (key_words, key_scales), slice(start, start + width))
+            return acc, slice(start, start + width)
+
+        def leave_psum(t):
+            gained = keep.tile([P, S], F32, name="a_gained%d" % t)
             rows = keep.tile([P, S], F32, name="a_rows%d" % t)
-            nc.scalar.copy(rows[:], acc[:])
+            for acc, cols in a_banks[t]:
+                nc.scalar.activation(gained[:, cols], acc[:], ACT.Copy, scale=ga_signed[:, t : t + 1])
+            for acc, cols in a_banks[t]:
+                nc.scalar.copy(rows[:, cols], acc[:])
+            a_gained.append(gained)
             a_rows.append(rows)
 
-        w2_bf = cast_weight(w2_raw, "w2")
+        z = keep.tile([P, PACK, S], F32, name="z")
 
-        z_codes = keep.tile([P, S], U32, name="z_codes", align_bytes=64)
-        z_scales = keep.tile([P, S], U8, name="z_scales", align_bytes=64)
+        def key_gathers(t):
+            name = "first%d" % t
+            first = keep.tile([P, S], F32, name=name, tag="w1_codes" if t == 2 else name, align_bytes=64)
+            for start in range(0, S, HALF):
+                nc.vector.tensor_copy(
+                    first[:, start : start + HALF], a_gained[t][:].indirect(list_slice(n1_list, start, HALF))
+                )
+            for start in range(0, S, HALF):
+                nc.vector.tensor_tensor(
+                    z[:, t, start : start + HALF],
+                    a_rows[t][:].indirect(list_slice(n2_list, start, HALF)),
+                    first[:, start : start + HALF],
+                    ALU.mult,
+                )
 
-        def key_gathers(c):
-            start, width = KEY_CHUNKS[c]
-            first = keep.tile([P, PACK, width], F32, name="first%d" % c, tag=("w1_bf", "w2_bf")[c], align_bytes=64)
-            z = keep.tile([P, PACK, width], F32, name="z%d" % c)
-            for pair in range(0, PACK, 2):
-                for t in (pair, pair + 1):
-                    nc.vector.tensor_tensor(
-                        first[:, t, :], a_rows[t][:].indirect(list_slice(n1_list, start, width)), ga_wide[:, t, :], ALU.mult
-                    )
-                for t in (pair, pair + 1):
-                    nc.vector.tensor_tensor(
-                        z[:, t, :], a_rows[t][:].indirect(list_slice(n2_list, start, width)), first[:, t, :], ALU.mult
-                    )
-            z_bf = keep.tile([P, width, PACK], BF16, name="z_bf%d" % c, tag="z_bf%d" % c, align_bytes=64)
-            nc.scalar.copy(interleaved(z_bf), by_planes(z))
-            return z_bf
+        a_banks = [[project_keys(0, 0, HALF, 0), project_keys(0, HALF, HALF, PACK)]]
+        a_banks.extend([project_keys(t, 0, S, t)] for t in range(1, PACK))
+        leave_psum(0)
+        leave_psum(1)
+        w2_bf = cast_weight(w2_raw, "w2_bf", "w1_codes", 0)
+        leave_psum(2)
+        leave_psum(3)
+        key_gathers(0)
+        key_gathers(1)
 
-        def key_quantize(c, z_bf):
-            start, width = KEY_CHUNKS[c]
-            cols = slice(start, start + width)
-            quantize(z_bf[:].rearrange("p c t -> p (c t)"), z_codes[:, cols], z_scales[:, cols])
-
-        z_bf0 = key_gathers(0)
-
-        w2_q = quantize_weight(w2_bf, "w2")
+        w2_q = quantize_weight(w2_bf, "w2", 1)
         b_rows = []
         b_own = []
         for t in range(PACK):
@@ -182,24 +200,29 @@ def tile_picked_keytwo_none_p_kernel(
             mx(acc[:], w2_q, slice(t * P, (t + 1) * P), (query_words, query_scales), slice(0, V))
             rows = keep.tile([P, V], F32, name="b_rows%d" % t)
             nc.scalar.activation(rows[:], acc[:], ACT.Copy, scale=gb_abs[:, t : t + 1])
-            own = keep.tile([P, V], F32, name="b_own%d" % t)
-            nc.sync.dma_start(own[:], rows[:])
+            own = []
+            for start in range(0, V, HALF):
+                half = keep.tile([P, HALF], F32, name="b_own%d_%d" % (t, start), tag="b_own%d_%d" % (t, start), align_bytes=64)
+                nc.sync.dma_start(half[:], rows[:, start : start + HALF])
+                own.append(half)
             b_rows.append(rows)
             b_own.append(own)
 
-        z_bf1 = key_gathers(1)
-        key_quantize(0, z_bf0)
+        key_gathers(2)
+        key_gathers(3)
+        z_bf = keep.tile([P, S, PACK], BF16, name="z_bf", tag="z_bf", align_bytes=64)
+        nc.scalar.copy(interleaved(z_bf), by_planes(z))
 
         out_rows = out.rearrange("(a p) v -> p a v", p=P)
 
         def query_gathers(c):
             start, width = QUERY_CHUNKS[c]
-            diff = keep.tile([P, PACK, width], F32, name="diff%d" % c, tag=("z_bf0", "z_bf1", "z2_bf0")[c], align_bytes=64)
+            diff = keep.tile([P, PACK, width], F32, name="diff%d" % c, tag=("diff0", "z_bf", "z2_bf0")[c], align_bytes=64)
             for t in range(PACK):
                 nc.vector.tensor_tensor(
                     diff[:, t, :],
                     b_rows[t][:].indirect(list_slice(nq_list, start, width)),
-                    b_own[t][:, start : start + width],
+                    b_own[t][start // HALF][:, start % HALF : start % HALF + width],
                     ALU.subtract,
                 )
             z2_bf = keep.tile([P, width, PACK], BF16, name="z2_bf%d" % c, tag="z2_bf%d" % c, align_bytes=64)
@@ -220,15 +243,18 @@ def tile_picked_keytwo_none_p_kernel(
                     rows = slice((2 * half + a) * P, (2 * half + a + 1) * P)
                     mx(acc[:, a, :], (z_codes, z_scales), rows, (codes, scales), slice(0, width))
                 name = "scores%d_%d" % (c, half)
-                scores = keep.tile([P, 2, width], F32, name=name, tag="z_bf1" if (c, half) == (0, 0) else name, align_bytes=64)
+                scores = keep.tile([P, 2, width], F32, name=name, tag=name, align_bytes=64)
                 if c == len(QUERY_CHUNKS) - 1 and half == 1:
                     nc.vector.tensor_scalar(scores[:], acc[:], 0.0625, None, ALU.mult)
                 else:
                     nc.scalar.activation(scores[:], acc[:], ACT.Copy, scale=0.0625)
-                nc.sync.dma_start(out_rows[:, 2 * half : 2 * half + 2, start : start + width], scores[:])
+                queue = nc.scalar if (c, half) == (len(QUERY_CHUNKS) - 1, 0) else nc.sync
+                queue.dma_start(out_rows[:, 2 * half : 2 * half + 2, start : start + width], scores[:])
 
         z2_bf0 = query_gathers(0)
-        key_quantize(1, z_bf1)
+        z_codes = keep.tile([P, S], U32, name="z_codes", align_bytes=64)
+        z_scales = keep.tile([P, S], U8, name="z_scales", tag="b_own3_0", align_bytes=64)
+        quantize(z_bf[:].rearrange("p c t -> p (c t)"), z_codes[:], z_scales[:])
         z2_bf1 = query_gathers(1)
         query_scores(0, z2_bf0)
         z2_bf2 = query_gathers(2)

from contextlib import ExitStack

import concourse.mybir as mybir

K, T, S, V, H = 512, 2048, 512, 512, 512
FLOPS = 2 * K * H * S + 2 * K * H * V + 2 * H * S * V

F32 = mybir.dt.float32
BF16 = mybir.dt.bfloat16
I32 = mybir.dt.int32
U32 = mybir.dt.uint32
U16 = mybir.dt.uint16
U8 = mybir.dt.uint8
FP8X4 = mybir.dt.float8_e4m3fn_x4
ALU = mybir.AluOpType
ACT = mybir.ActivationFunctionType

P = 128
PACK = 4
LIST_ROWS = 16
HALF = 256
KEY_CHUNKS = ((0, 256), (256, 256))
QUERY_CHUNKS = ((0, 256), (256, 128), (384, 128))


def list_slice(offsets, start, width):
    return offsets[:, start // LIST_ROWS : (start + width) // LIST_ROWS]


def interleaved(tile):
    return tile[:].rearrange("p (c i) t -> p c t i", i=4)


def by_planes(tile):
    return tile[:].rearrange("p t (c i) -> p c t i", i=4)


def tile_picked_keytwo_none_p_kernel(
    tc, x_words, x_scales, w1, w2, ga, gb, offs, two, n1, n2, nq, out
):
    nc = tc.nc
    with ExitStack() as ctx:
        lists = ctx.enter_context(tc.tile_pool(name="lists", bufs=1))
        keep = ctx.enter_context(tc.tile_pool(name="keep", bufs=1))
        psum = ctx.enter_context(tc.psum_pool(name="psum", bufs=1))

        def load_list(source, name):
            tile = lists.tile([P, S // LIST_ROWS], U16, name=name)
            nc.sync.dma_start(tile[:], source)
            return tile

        def load_weight_half(w, name, h):
            rows = w.rearrange("(p j) c -> p j c", j=PACK)
            raw = keep.tile([P, PACK, HALF], F32, name="%s_raw%d" % (name, h))
            nc.sync.dma_start(raw[:], rows[:, :, h * HALF : (h + 1) * HALF])
            return raw

        def load_gain(g, name):
            tile = keep.tile([P, PACK], F32, name=name)
            nc.sync.dma_start(tile[:], g.rearrange("(p t) o -> p (t o)", t=PACK))
            return tile

        def cast_weight(halves, name, tag, vector_columns):
            grouped = keep.tile([P, PACK, P, PACK], BF16, name=name, tag=tag, align_bytes=64)

            def cast(copy, first, last):
                h, start = divmod(first, HALF)
                copy(
                    grouped[:, :, first // PACK : last // PACK, :].rearrange("p t m j -> p m j t"),
                    halves[h][:, :, start : start + last - first].rearrange("p j (m t) -> p m j t", t=PACK),
                )

            cast(nc.scalar.copy, 0, HALF)
            cast(nc.scalar.copy, HALF, H - vector_columns)
            if vector_columns:
                cast(nc.vector.tensor_copy, H - vector_columns, H)
            return grouped

        def quantize(grouped_flat, codes, scales):
            nc.vector.quantize_mx(out=codes.bitcast(FP8X4), scales=scales, in_=grouped_flat)

        def quantize_weight(grouped, name, calls):
            codes = keep.tile([P, H], U32, name=name + "_codes", tag=name + "_codes", align_bytes=64)
            scales = keep.tile([P, H], U8, name=name + "_scales", align_bytes=64)
            flat = grouped[:].rearrange("p t m j -> p (t m j)")
            width = H // calls
            for c in range(0, H, width):
                quantize(flat[:, PACK * c : PACK * (c + width)], codes[:, c : c + width], scales[:, c : c + width])
            return codes, scales

        def mx(acc, lhs, lhs_cols, rhs, rhs_cols):
            nc.tensor.matmul_mx(
                out=acc,
                lhsT=lhs[0][:, lhs_cols].bitcast(FP8X4),
                lhsT_scale=lhs[1][:, lhs_cols],
                rhs=rhs[0][:, rhs_cols].bitcast(FP8X4),
                rhs_scale=rhs[1][:, rhs_cols],
                start=True,
                stop=True,
            )

        table_scales = keep.tile([P, T], U8, name="table_scales")
        nc.vector.memset(table_scales[:].bitcast(I32), 0)
        offs_list = load_list(offs, "offs_list")
        two_list = load_list(two, "two_list")
        w1_raw = [load_weight_half(w1, "w1", 0)]
        for q in range(4):
            nc.sync.dma_start(
                table_scales[32 * q : 32 * q + 4, :].bitcast(I32),
                x_scales[0, 4 * q : 4 * q + 4, :].bitcast(I32),
            )
        w1_raw.append(load_weight_half(w1, "w1", 1))
        gb_raw = load_gain(gb, "gb_raw")
        table_words = keep.tile([P, T], U32, name="table_words")
        nc.sync.dma_start(
            table_words[:].bitcast(I32), x_words[0].rearrange("p n t -> p (n t)").bitcast(I32)
        )
        ga_raw = load_gain(ga, "ga_raw")
        n1_list = load_list(n1, "n1_list")
        n2_list = load_list(n2, "n2_list")
        w2_raw = [load_weight_half(w2, "w2", h) for h in range(2)]
        nq_list = load_list(nq, "nq_list")

        def pick(table, dtype, offsets, name, calls):
            picked = keep.tile([P, S], dtype, name=name, align_bytes=64)
            width = S // calls
            for start in range(0, S, width):
                nc.vector.tensor_copy(
                    picked[:, start : start + width], table[:].indirect(list_slice(offsets, start, width))
                )
            return picked

        key_scales = pick(table_scales, U8, offs_list, "key_scales", 1)
        query_scales = pick(table_scales, U8, two_list, "query_scales", 1)
        w1_q = quantize_weight(cast_weight(w1_raw, "w1_bf", "w1_bf", 0), "w1", 1)
        key_words = pick(table_words, U32, offs_list, "key_words", 2)
        query_words = pick(table_words, U32, two_list, "query_words", 1)

        sign3 = keep.tile([P, PACK], F32, name="sign3")
        sign = keep.tile([P, PACK], F32, name="sign")
        gb_abs = keep.tile([P, PACK], F32, name="gb_abs")
        nc.scalar.activation(sign3[:], gb_raw[:], ACT.Sign)
        nc.scalar.activation(gb_abs[:], gb_raw[:], ACT.Abs)
        nc.scalar.activation(sign[:], sign3[:], ACT.Sign, bias=1.0, scale=2.0)
        ga_signed = keep.tile([P, PACK], F32, name="ga_signed")
        for t in range(PACK):
            nc.scalar.activation(ga_signed[:, t : t + 1], ga_raw[:, t : t + 1], ACT.Copy, scale=sign[:, t : t + 1])


        a_rows = []
        a_gained = []

        def project_keys(t, start, width, bank):
            acc = psum.tile([P, width], F32, name="acc_a%d_%d" % (t, start), tag="bank%d" % bank)
            mx(acc[:], w1_q, slice(t * P, (t + 1) * P), (key_words, key_scales), slice(start, start + width))
            return acc, slice(start, start + width)

        def leave_psum(t):
            gained = keep.tile([P, S], F32, name="a_gained%d" % t)
            rows = keep.tile([P, S], F32, name="a_rows%d" % t)
            for acc, cols in a_banks[t]:
                nc.scalar.activation(gained[:, cols], acc[:], ACT.Copy, scale=ga_signed[:, t : t + 1])
            for acc, cols in a_banks[t]:
                nc.scalar.copy(rows[:, cols], acc[:])
            a_gained.append(gained)
            a_rows.append(rows)

        z = keep.tile([P, PACK, S], F32, name="z")

        def key_gathers(t):
            name = "first%d" % t
            first = keep.tile([P, S], F32, name=name, tag="w1_codes" if t == 2 else name, align_bytes=64)
            for start in range(0, S, HALF):
                nc.vector.tensor_copy(
                    first[:, start : start + HALF], a_gained[t][:].indirect(list_slice(n1_list, start, HALF))
                )
            for start in range(0, S, HALF):
                nc.vector.tensor_tensor(
                    z[:, t, start : start + HALF],
                    a_rows[t][:].indirect(list_slice(n2_list, start, HALF)),
                    first[:, start : start + HALF],
                    ALU.mult,
                )

        a_banks = [[project_keys(0, 0, HALF, 0), project_keys(0, HALF, HALF, PACK)]]
        a_banks.extend([project_keys(t, 0, S, t)] for t in range(1, PACK))
        leave_psum(0)
        leave_psum(1)
        w2_bf = cast_weight(w2_raw, "w2_bf", "w1_codes", 0)
        leave_psum(2)
        leave_psum(3)
        key_gathers(0)
        key_gathers(1)

        w2_q = quantize_weight(w2_bf, "w2", 1)
        b_rows = []
        b_own = []
        for t in range(PACK):
            acc = psum.tile([P, V], F32, name="acc_b%d" % t, tag="bank%d" % (PACK + t))
            mx(acc[:], w2_q, slice(t * P, (t + 1) * P), (query_words, query_scales), slice(0, V))
            rows = keep.tile([P, V], F32, name="b_rows%d" % t)
            nc.scalar.activation(rows[:], acc[:], ACT.Copy, scale=gb_abs[:, t : t + 1])
            own = []
            for start in range(0, V, HALF):
                half = keep.tile([P, HALF], F32, name="b_own%d_%d" % (t, start), tag="b_own%d_%d" % (t, start), align_bytes=64)
                nc.sync.dma_start(half[:], rows[:, start : start + HALF])
                own.append(half)
            b_rows.append(rows)
            b_own.append(own)

        key_gathers(2)
        key_gathers(3)
        z_bf = keep.tile([P, S, PACK], BF16, name="z_bf", tag="z_bf", align_bytes=64)
        nc.scalar.copy(interleaved(z_bf), by_planes(z))

        out_rows = out.rearrange("(a p) v -> p a v", p=P)

        def query_gathers(c):
            start, width = QUERY_CHUNKS[c]
            diff = keep.tile([P, PACK, width], F32, name="diff%d" % c, tag=("diff0", "z_bf", "z2_bf0")[c], align_bytes=64)
            for t in range(PACK):
                nc.vector.tensor_tensor(
                    diff[:, t, :],
                    b_rows[t][:].indirect(list_slice(nq_list, start, width)),
                    b_own[t][start // HALF][:, start % HALF : start % HALF + width],
                    ALU.subtract,
                )
            z2_bf = keep.tile([P, width, PACK], BF16, name="z2_bf%d" % c, tag="z2_bf%d" % c, align_bytes=64)
            if c == len(QUERY_CHUNKS) - 1:
                nc.vector.tensor_scalar(interleaved(z2_bf), by_planes(diff), 0.0, None, ALU.max)
            else:
                nc.scalar.activation(interleaved(z2_bf), by_planes(diff), ACT.Relu)
            return z2_bf

        def query_scores(c, z2_bf):
            start, width = QUERY_CHUNKS[c]
            codes = keep.tile([P, width], U32, name="z2_codes%d" % c, align_bytes=64)
            scales = keep.tile([P, width], U8, name="z2_scales%d" % c, align_bytes=64)
            quantize(z2_bf[:].rearrange("p c t -> p (c t)"), codes[:], scales[:])
            for half in range(2):
                acc = psum.tile([P, 2, width], F32, name="acc_s%d_%d" % (c, half), tag="bank%d" % (2 * c + half))
                for a in range(2):
                    rows = slice((2 * half + a) * P, (2 * half + a + 1) * P)
                    mx(acc[:, a, :], (z_codes, z_scales), rows, (codes, scales), slice(0, width))
                name = "scores%d_%d" % (c, half)
                scores = keep.tile([P, 2, width], F32, name=name, tag=name, align_bytes=64)
                if c == len(QUERY_CHUNKS) - 1 and half == 1:
                    nc.vector.tensor_scalar(scores[:], acc[:], 0.0625, None, ALU.mult)
                else:
                    nc.scalar.activation(scores[:], acc[:], ACT.Copy, scale=0.0625)
                queue = nc.scalar if (c, half) == (len(QUERY_CHUNKS) - 1, 0) else nc.sync
                queue.dma_start(out_rows[:, 2 * half : 2 * half + 2, start : start + width], scores[:])

        z2_bf0 = query_gathers(0)
        z_codes = keep.tile([P, S], U32, name="z_codes", align_bytes=64)
        z_scales = keep.tile([P, S], U8, name="z_scales", tag="b_own3_0", align_bytes=64)
        quantize(z_bf[:].rearrange("p c t -> p (c t)"), z_codes[:], z_scales[:])
        z2_bf1 = query_gathers(1)
        query_scores(0, z2_bf0)
        z2_bf2 = query_gathers(2)
        query_scores(1, z2_bf1)
        query_scores(2, z2_bf2)
